import numpy as np
import ml_dtypes


def mxq(x, axis, fmt="e4m3"):
    dtype, down = {"e4m3": (ml_dtypes.float8_e4m3fn, 7), "e5m2": (ml_dtypes.float8_e5m2, 14)}[fmt]
    v = np.moveaxis(np.asarray(x, np.float32).astype(ml_dtypes.bfloat16).astype(np.float64), axis, -1)
    blocks = v.reshape(v.shape[:-1] + (-1, 32))
    amax = np.abs(blocks).max(-1, keepdims=True)
    byte = np.maximum(np.where(amax > 0, np.frexp(amax)[1] - 1 + 127, 0) - down, 1)
    scale = np.exp2(byte - 127.0)
    codes = (blocks / scale).astype(np.float32).astype(dtype).astype(np.float64)
    return np.moveaxis((codes * scale).reshape(v.shape), -1, axis)


WIDE = False


def mx_kscale(k):
    if not WIDE:
        return np.ones(k)
    levels = np.array([10, -10, 5, -5, 0])
    if k % 512:
        return np.exp2(np.random.permutation(np.resize(levels, k // 32))).repeat(32)
    a = np.empty((k // 512, 16))
    for p in range(k // 512):
        a[p, :8] = np.random.permutation(np.resize(levels, 8))
        for g in range(8):
            far = levels[np.abs(levels - a[p, g]) >= 10]
            a[p, g + 8] = far[np.random.randint(len(far))]
    return np.exp2(a.ravel()).repeat(32)


def f64(x):
    return np.asarray(x).astype(np.float64)


def striped(idx):
    return np.tile(idx.reshape(-1, 16).T, (8, 1)).astype(np.uint16)


def unstriped(offs):
    return offs[:16].T.reshape(-1).astype(np.int64)


E2M1 = np.array([0.0, 0.5, 1.0, 1.5, 2.0, 3.0, 4.0, 6.0, -0.0, -0.5, -1.0, -1.5, -2.0, -3.0, -4.0, -6.0])


def pack_weight(w, fmt):
    k, n = w.shape
    w = f64(np.asarray(w, np.float32).astype(ml_dtypes.bfloat16)).reshape(k // 32, 32, n)
    amax = np.abs(w).max(1)
    if fmt == "e4m3":
        byte = np.frexp(amax)[1] - 1 + 127 - 7
    else:
        mant, ex = np.frexp(amax / 6.0)
        byte = np.where(mant > 0.5, ex, ex - 1) + 127
    byte = np.clip(np.where(amax > 0, byte, 1), 1, 254)
    scaled = (w * np.exp2(127.0 - byte)[:, None, :]).reshape(k, n).astype(np.float32)
    by_word = np.ascontiguousarray(scaled.reshape(k // 512, 128, 4, n).transpose(0, 1, 3, 2))
    if fmt == "e4m3":
        words = by_word.astype(ml_dtypes.float8_e4m3fn).view(np.uint8)
    else:
        c = by_word.astype(ml_dtypes.float4_e2m1fn).view(np.uint8) & 0xF
        words = (c[..., 0::2] | (c[..., 1::2] << 4)).reshape(k // 512, 128, 2 * n)
    return np.ascontiguousarray(words), np.ascontiguousarray(byte.astype(np.uint8).reshape(k // 512, 16, n))


def unpack_weight(words, scales, fmt):
    g, _, n = scales.shape
    words = np.ascontiguousarray(words).reshape(g, 128, n, -1)
    if fmt == "e4m3":
        vals = words.view(ml_dtypes.float8_e4m3fn).astype(np.float64)
    else:
        nib = np.empty((g, 128, n, 4), np.uint8)
        nib[..., 0::2] = words & 0xF
        nib[..., 1::2] = words >> 4
        vals = E2M1[nib]
    vals = vals * np.repeat(np.exp2(scales.astype(np.float64) - 127.0), 8, axis=1)[..., None]
    return vals.transpose(0, 1, 3, 2).reshape(g * 512, n)


def relu(v):
    return np.maximum(v, 0.0)


K, T, E, C, H, N = 1024, 640, 15, 128, 512, 128
TOP = 3


def by_expert(wq, xq):
    return np.concatenate([wq[e].T @ xq[:, e * C:(e + 1) * C] for e in range(E)], axis=1)


def setup_inputs():
    n = np.random.standard_normal
    s = mx_kscale(K)[:, None]
    u = mx_kscale(H)
    deal = np.repeat(np.arange(E), C).reshape(TOP, T)[:, np.random.permutation(T)]
    deal = np.take_along_axis(deal, np.argsort(np.random.rand(TOP, T), axis=0), axis=0)
    for _ in range(8):
        s_, t_ = np.random.permutation(T).reshape(2, -1); r = np.random.randint(TOP, size=T // 2); x, y = deal[r, s_].copy(), deal[r, t_].copy()
        ok = ~((deal[:, s_] == y).any(0) | (deal[:, t_] == x).any(0)); deal[r[ok], s_[ok]] = y[ok]; deal[r[ok], t_[ok]] = x[ok]
    order = np.lexsort((np.random.rand(TOP * T), deal.reshape(-1)))
    slot_token = order % T; pos = np.empty(TOP * T, np.int64); pos[order] = np.arange(TOP * T); pos = pos.reshape(TOP, T)
    g = np.random.uniform(0.5, 1.5, (TOP, T)); g = g / g.sum(0)
    w1 = [pack_weight(m, "e2m1") for m in n((E, K, H)) / np.sqrt(K) / s[None] * u[None, None, :]]
    w2 = [pack_weight(m, "e2m1") for m in n((E, H, N)) / np.sqrt(H) / u[None, :, None]]
    return {
        "xT": (n((K, T)) * s).astype(np.float32),
        "w1_words": np.stack([m[0] for m in w1]),
        "w1_scales": np.stack([m[1] for m in w1]),
        "w2_words": np.stack([m[0] for m in w2]),
        "w2_scales": np.stack([m[1] for m in w2]),
        "gate": np.stack([np.tile(r, (N, 1)) for r in g]).astype(np.float32),
        "offs": striped(slot_token),
        "pos1": striped(pos[0]),
        "pos2": striped(pos[1]),
        "pos3": striped(pos[2]),
    }


def reference(xT, w1_words, w1_scales, w2_words, w2_scales, gate, offs, pos1, pos2, pos3):
    idx = unstriped(offs)
    w1 = np.stack([unpack_weight(w1_words[e], w1_scales[e], "e2m1") for e in range(E)])
    w2 = np.stack([unpack_weight(w2_words[e], w2_scales[e], "e2m1") for e in range(E)])
    xq = mxq(f64(xT)[:, idx], 0, "e4m3")
    h = relu(by_expert(w1, xq))
    y = by_expert(w2, mxq(h, 0, "e4m3"))
    return sum(f64(gate[r]) * y[:, unstriped(p)] for r, p in enumerate((pos1, pos2, pos3)))

@@ -1,0 +1,236 @@
+from contextlib import ExitStack
+
+import concourse.mybir as mybir
+from concourse.masks import make_identity
+
+F32 = mybir.dt.float32
+BF16 = mybir.dt.bfloat16
+I32 = mybir.dt.int32
+U32 = mybir.dt.uint32
+U16 = mybir.dt.uint16
+U8 = mybir.dt.uint8
+FP8X4 = mybir.dt.float8_e4m3fn_x4
+FP4X4 = mybir.dt.float4_e2m1fn_x4
+ACT = mybir.ActivationFunctionType
+MULT = mybir.AluOpType.mult
+ADD = mybir.AluOpType.add
+
+P = 128
+K, T, E, C, H, N = 1024, 640, 15, 128, 512, 128
+TOP = 3
+S = E * C
+PASSES = K // 512
+FLOPS = 2 * S * H * (K + N)
+
+CHUNKS = ((0, 2), (2, 5), (5, 8), (8, 11), (11, 14), (14, 15))
+W_LOADS = ((0, 2), (2, 5), (5, 8), (8, 11), (11, 15))
+SHIFTS = {0: (0, 2), 2: (2, 8), 5: (8, 15)}
+GROUPS = ((0, 2), (2, 4), (4, 6), (6, 8), (8, 10), (10, 12), (12, 14), (14, 15))
+VECTOR_TURNS = (2, 6, 10)
+T_LOADS = ((0, 256), (256, 640))
+T_PARTS = ((0, 256), (256, 512), (512, 640))
+
+
+def tile_moe_tk_mlp_relu_kernel(tc, xT, w1_words, w1_scales, w2_words, w2_scales, gate, offs, pos1, pos2, pos3, out):
+    nc = tc.nc
+    with ExitStack() as ctx:
+        lists = ctx.enter_context(tc.tile_pool(name="lists", bufs=1))
+        keep = ctx.enter_context(tc.tile_pool(name="keep", bufs=1))
+        wring = ctx.enter_context(tc.tile_pool(name="wring", bufs=3))
+        ring = ctx.enter_context(tc.tile_pool(name="ring", bufs=4))
+        psum_a = ctx.enter_context(tc.psum_pool(name="psum_a", bufs=4))
+        psum_t = ctx.enter_context(tc.psum_pool(name="psum_t", bufs=2))
+        psum_y = ctx.enter_context(tc.psum_pool(name="psum_y", bufs=2))
+
+        offs_t = lists.tile([P, S // 16], U16, name="offs_t")
+        pos_t = [lists.tile([P, T // 16], U16, name="pos_t%d" % r) for r in range(TOP)]
+
+        x_view = xT.rearrange("(s p j) t -> s p j t", p=P, j=4)
+        x_raw = {}
+        for s in range(PASSES):
+            for a, b in T_LOADS:
+                raw = keep.tile([P, 4, b - a], F32, name="x_raw_%d_%d" % (s, a))
+                nc.sync.dma_start(out=raw[:], in_=x_view[s, :, :, a:b])
+                x_raw[s, a] = raw
+            if s == 0:
+                nc.sync.dma_start(offs_t[:], offs)
+                for r, pos in enumerate((pos1, pos2, pos3)):
+                    nc.sync.dma_start(pos_t[r][:], pos)
+
+        w1s = keep.tile([P, E * PASSES * H], U8, align_bytes=64, name="w1s")
+        w2s = keep.tile([P, E * N], U8, align_bytes=64, name="w2s")
+        nc.vector.memset(w1s[:].bitcast(I32), 0)
+        nc.vector.memset(w2s[:].bitcast(I32), 0)
+        xs = keep.tile([P, T], U8, align_bytes=64, name="xs")
+        nc.gpsimd.memset(xs[:], 0)
+        gs1 = keep.tile([P, S], U8, align_bytes=64, name="gs1")
+        nc.gpsimd.memset(gs1[:], 0)
+        ident = keep.tile([P, P], F32, name="ident")
+        make_identity(nc, ident[:])
+
+        w1 = {}
+        w1_view = w1_words.rearrange("e s p b -> p e s b").bitcast(I32)
+        w1s_view = w1_scales.rearrange("e s q i -> q (e s) i").bitcast(I32)
+        w2s_view = w2_scales.rearrange("e s q n -> q (e s) n").bitcast(I32)
+        def load_w1(a, b):
+            w = wring.tile([P, 4, PASSES, 2 * H], U8, align_bytes=64, tag="w1", name="w1")
+            nc.sync.dma_start(out=w[:, : b - a].bitcast(I32), in_=w1_view[:, a:b])
+            for e in range(a, b):
+                w1[e] = (w, e - a)
+
+        load_w1(*W_LOADS[0])
+        for q in range(4):
+            nc.sync.dma_start(
+                out=w1s[32 * q : 32 * q + 4, :].bitcast(I32).rearrange("q (a i) -> q a i", i=H // 4),
+                in_=w1s_view[4 * q : 4 * q + 4, :, :],
+            )
+        for q in range(4):
+            nc.gpsimd.dma_start(
+                out=w2s[32 * q : 32 * q + 4, :].bitcast(I32).rearrange("q (a n) -> q a n", n=N // 4),
+                in_=w2s_view[4 * q : 4 * q + 4, :, :],
+            )
+        def load_rest():
+            nc.sync.dma_start(out=w2[:].bitcast(I32), in_=w2_words.rearrange("e s p b -> p (e s) b").bitcast(I32))
+
+        w2 = keep.tile([P, E, 2 * N], U8, align_bytes=64, name="w2")
+
+        xw = [keep.tile([P, T], U32, align_bytes=64, name="xw%d" % s) for s in range(PASSES)]
+        gw = [keep.tile([P, S], U32, align_bytes=64, name="gw%d" % s) for s in range(PASSES)]
+        gs = keep.tile([P, S], U8, align_bytes=64, name="gs")
+
+        def interleave(s, i, engine):
+            a, b = T_PARTS[i]
+            load = max(l[0] for l in T_LOADS if l[0] <= a)
+            raw = x_raw[s, load]
+            xb = keep.tile([P, b - a, 4], BF16, align_bytes=64, name="xb_%d_%d" % (s, a))
+            src = raw[:, :, a - load : b - load].rearrange("p j t -> p t j")
+            if engine == "v":
+                nc.vector.tensor_copy(out=xb[:], in_=src)
+            else:
+                nc.scalar.copy(out=xb[:], in_=src)
+            return xb
+
+        def quantise_x(s, i, xb):
+            a, b = T_PARTS[i]
+            nc.vector.quantize_mx(
+                out=xw[s][:, a:b].bitcast(FP8X4),
+                scales=xs[4 * s : P, a:b],
+                in_=xb[:].rearrange("p t j -> p (t j)"),
+            )
+
+        def gather_words(s, c):
+            a, b = CHUNKS[c][0] * C, CHUNKS[c][1] * C
+            nc.vector.tensor_copy(out=gw[s][:, a:b], in_=xw[s][:].indirect(offs_t[:, a // 16 : b // 16]))
+
+        def gather_scales(c):
+            a, b = CHUNKS[c][0] * C, CHUNKS[c][1] * C
+            nc.vector.tensor_copy(out=gs[:, a:b], in_=xs[:].indirect(offs_t[:, a // 16 : b // 16]))
+            if CHUNKS[c][1] in [x[1] for x in SHIFTS.values()]:
+                lo = [x for x in SHIFTS.values() if x[1] == CHUNKS[c][1]][0][0] * C
+                for q in range(4):
+                    nc.scalar.dma_start(
+                        out=gs1[32 * q : 32 * q + 4, lo:b].bitcast(I32),
+                        in_=gs[32 * q + 4 : 32 * q + 8, lo:b].bitcast(I32),
+                    )
+
+        for s, engines in ((0, "vsv"), (1, "svs")):
+            xbs = [interleave(s, i, engines[i]) for i in range(3)]
+            for i in range(3):
+                quantise_x(s, i, xbs[i])
+            if s == 0:
+                gather_words(0, 0)
+        gather_scales(0)
+        gather_words(1, 0)
+        load_rest()
+        load_w1(*W_LOADS[1])
+        gather_scales(1)
+        gather_scales(2)
+        gather_words(0, 1)
+        load_w1(*W_LOADS[2])
+        gather_words(1, 1)
+        scaled = 3
+
+        y_all = keep.tile([P, S], F32, name="y_all")
+
+        def experts(a, b):
+            n = b - a
+            ht = psum_t.tile([P, n, 2, C], F32, name="ht")
+            for e in range(a, b):
+                acc = psum_a.tile([C, H], F32, name="acc")
+                w, at = w1[e]
+                slots = slice(e * C, (e + 1) * C)
+                for s in range(PASSES):
+                    cols = slice((e * PASSES + s) * H, (e * PASSES + s + 1) * H)
+                    nc.tensor.matmul_mx(
+                        out=acc[:],
+                        lhsT=gw[s][:, slots].bitcast(FP8X4),
+                        lhsT_scale=(gs, gs1)[s][:, slots],
+                        rhs=w[:, at, s, :].bitcast(FP4X4),
+                        rhs_scale=w1s[:, cols],
+                        start=(s == 0),
+                        stop=(s == PASSES - 1),
+                    )
+                h = ring.tile([C, 2, P, 2], BF16, name="h")
+                nc.scalar.activation(out=h[:], in_=acc[:].rearrange("c (p u d) -> c u p d", u=2, d=2), func=ACT.Relu)
+                pairs = h[:].rearrange("c u p d -> c (u p d)").bitcast(F32)
+                for u in range(2):
+                    nc.tensor.transpose(ht[:, e - a, u, :], pairs[:, u * P : (u + 1) * P], ident[:])
+            hb = ring.tile([P, n * C, 4], BF16, align_bytes=64, name="hb")
+            copy = nc.vector.tensor_copy if a in VECTOR_TURNS else nc.scalar.copy
+            copy(
+                out=hb[:].rearrange("p c d -> p (c d)").bitcast(F32).rearrange("p (g c u) -> p g c u", g=n, u=2),
+                in_=ht[:].rearrange("p g u c -> p g c u"),
+            )
+            hw = ring.tile([P, n * C], U32, align_bytes=64, name="hw")
+            hs = ring.tile([P, n * C], U8, align_bytes=64, name="hs")
+            nc.vector.quantize_mx(out=hw[:].bitcast(FP8X4), scales=hs[:], in_=hb[:].rearrange("p c d -> p (c d)"))
+            y = psum_y.tile([N, n * C], F32, name="y")
+            for e in range(a, b):
+                cols = slice((e - a) * C, (e - a + 1) * C)
+                nc.tensor.matmul_mx(
+                    out=y[:, cols],
+                    lhsT=w2[:, e, :].bitcast(FP4X4),
+                    lhsT_scale=w2s[:, e * N : (e + 1) * N],
+                    rhs=hw[:, cols].bitcast(FP8X4),
+                    rhs_scale=hs[:, cols],
+                    start=True,
+                    stop=True,
+                )
+            nc.scalar.copy(out=y_all[:, a * C : b * C], in_=y[:])
+
+        gathered = 2
+        loaded = 3
+        for a, b in GROUPS:
+            while gathered < len(CHUNKS) and CHUNKS[gathered - 1][0] <= b:
+                while scaled < len(CHUNKS) and scaled <= gathered + 3:
+                    gather_scales(scaled)
+                    scaled += 1
+                gather_words(0, gathered)
+                gather_words(1, gathered)
+                gathered += 1
+            if loaded < len(W_LOADS) and W_LOADS[loaded - 2][0] <= a:
+                load_w1(*W_LOADS[loaded])
+                loaded += 1
+            if a == 10:
+                gates = wring.tile([P, TOP, T], F32, align_bytes=64, tag="w1", name="gates")
+                nc.sync.dma_start(out=gates[:], in_=gate.rearrange("r n t -> n r t"))
+            experts(a, b)
+
+        half = T // 2
+        for i in range(2):
+            t = slice(i * half, (i + 1) * half)
+            prods = []
+            for r in range(TOP):
+                prod = keep.tile([N, half], F32, name="prod_%d_%d" % (i, r))
+                nc.vector.tensor_tensor(
+                    out=prod[:],
+                    in0=y_all[:].indirect(pos_t[r][:, i * half // 16 : (i + 1) * half // 16]),
+                    in1=gates[:, r, t],
+                    op=MULT,
+                )
+                prods.append(prod)
+            part = keep.tile([N, half], F32, name="part_%d" % i)
+            nc.vector.tensor_tensor(out=part[:], in0=prods[0][:], in1=prods[1][:], op=ADD)
+            result = keep.tile([N, half], F32, name="result_%d" % i)
+            nc.vector.tensor_tensor(out=result[:], in0=part[:], in1=prods[2][:], op=ADD)
+            nc.sync.dma_start(out=out[:, t], in_=result[:])

@@ -26,7 +26,8 @@ CHUNKS = ((0, 2), (2, 5), (5, 8), (8, 11), (11, 14), (14, 15))
 W_LOADS = ((0, 2), (2, 5), (5, 8), (8, 11), (11, 15))
 SHIFTS = {0: (0, 2), 2: (2, 8), 5: (8, 15)}
 GROUPS = ((0, 2), (2, 4), (4, 6), (6, 8), (8, 10), (10, 12), (12, 14), (14, 15))
-VECTOR_TURNS = (2, 6, 10)
+VECTOR_TURNS = (4, 8, 12)
+S_LOADS = ((0, 5), (5, 15))
 T_LOADS = ((0, 256), (256, 640))
 T_PARTS = ((0, 256), (256, 512), (512, 640))
 
@@ -36,7 +37,7 @@ def tile_moe_tk_mlp_relu_kernel(tc, xT, w1_words, w1_scales, w2_words, w2_scales
     with ExitStack() as ctx:
         lists = ctx.enter_context(tc.tile_pool(name="lists", bufs=1))
         keep = ctx.enter_context(tc.tile_pool(name="keep", bufs=1))
-        wring = ctx.enter_context(tc.tile_pool(name="wring", bufs=3))
+        wring = ctx.enter_context(tc.tile_pool(name="wring", bufs=4))
         ring = ctx.enter_context(tc.tile_pool(name="ring", bufs=4))
         psum_a = ctx.enter_context(tc.psum_pool(name="psum_a", bufs=4))
         psum_t = ctx.enter_context(tc.psum_pool(name="psum_t", bufs=2))
@@ -45,51 +46,59 @@ def tile_moe_tk_mlp_relu_kernel(tc, xT, w1_words, w1_scales, w2_words, w2_scales
         offs_t = lists.tile([P, S // 16], U16, name="offs_t")
         pos_t = [lists.tile([P, T // 16], U16, name="pos_t%d" % r) for r in range(TOP)]
 
+        w1s = {}
+        for a, b in S_LOADS:
+            w1s[a] = keep.tile([P, (b - a) * PASSES * H], U8, align_bytes=64, name="w1s_%d" % a)
+        w2s = keep.tile([P, E * N], U8, align_bytes=64, name="w2s")
+        xs = keep.tile([P, T], U8, align_bytes=64, name="xs")
+        gs1 = keep.tile([P, S], U8, align_bytes=64, name="gs1")
+        for t in (w1s[0], w1s[S_LOADS[1][0]], xs, w2s, gs1):
+            nc.vector.memset(t[:].bitcast(I32), 0)
+
+        w1s_view = w1_scales.rearrange("e s q i -> q (e s) i").bitcast(I32)
+
+        def load_w1s(a, b):
+            for q in range(4):
+                nc.sync.dma_start(
+                    out=w1s[a][32 * q : 32 * q + 4, :].bitcast(I32).rearrange("q (a i) -> q a i", i=H // 4),
+                    in_=w1s_view[4 * q : 4 * q + 4, a * PASSES : b * PASSES, :],
+                )
+
         x_view = xT.rearrange("(s p j) t -> s p j t", p=P, j=4)
         x_raw = {}
         for s in range(PASSES):
             for a, b in T_LOADS:
-                raw = keep.tile([P, 4, b - a], F32, name="x_raw_%d_%d" % (s, a))
+                raw = wring.tile([P, 4, b - a], F32, align_bytes=64, tag="big", name="x_raw_%d_%d" % (s, a))
                 nc.sync.dma_start(out=raw[:], in_=x_view[s, :, :, a:b])
                 x_raw[s, a] = raw
             if s == 0:
                 nc.sync.dma_start(offs_t[:], offs)
-                for r, pos in enumerate((pos1, pos2, pos3)):
-                    nc.sync.dma_start(pos_t[r][:], pos)
-
-        w1s = keep.tile([P, E * PASSES * H], U8, align_bytes=64, name="w1s")
-        w2s = keep.tile([P, E * N], U8, align_bytes=64, name="w2s")
-        nc.vector.memset(w1s[:].bitcast(I32), 0)
-        nc.vector.memset(w2s[:].bitcast(I32), 0)
-        xs = keep.tile([P, T], U8, align_bytes=64, name="xs")
-        nc.gpsimd.memset(xs[:], 0)
-        gs1 = keep.tile([P, S], U8, align_bytes=64, name="gs1")
-        nc.gpsimd.memset(gs1[:], 0)
-        ident = keep.tile([P, P], F32, name="ident")
-        make_identity(nc, ident[:])
 
         w1 = {}
         w1_view = w1_words.rearrange("e s p b -> p e s b").bitcast(I32)
-        w1s_view = w1_scales.rearrange("e s q i -> q (e s) i").bitcast(I32)
         w2s_view = w2_scales.rearrange("e s q n -> q (e s) n").bitcast(I32)
         def load_w1(a, b):
-            w = wring.tile([P, 4, PASSES, 2 * H], U8, align_bytes=64, tag="w1", name="w1")
+            if a == 0:
+                w = keep.tile([P, b - a, PASSES, 2 * H], U8, align_bytes=64, name="w1_first")
+            else:
+                w = wring.tile([P, 4, PASSES, 2 * H], U8, align_bytes=64, tag="big", name="w1")
             nc.sync.dma_start(out=w[:, : b - a].bitcast(I32), in_=w1_view[:, a:b])
             for e in range(a, b):
                 w1[e] = (w, e - a)
 
         load_w1(*W_LOADS[0])
+        load_w1s(*S_LOADS[0])
+        for r, pos in enumerate((pos1, pos2, pos3)):
+            nc.sync.dma_start(pos_t[r][:], pos)
+        ident = keep.tile([P, P], F32, name="ident")
+        make_identity(nc, ident[:])
         for q in range(4):
             nc.sync.dma_start(
-                out=w1s[32 * q : 32 * q + 4, :].bitcast(I32).rearrange("q (a i) -> q a i", i=H // 4),
-                in_=w1s_view[4 * q : 4 * q + 4, :, :],
-            )
-        for q in range(4):
-            nc.gpsimd.dma_start(
                 out=w2s[32 * q : 32 * q + 4, :].bitcast(I32).rearrange("q (a n) -> q a n", n=N // 4),
                 in_=w2s_view[4 * q : 4 * q + 4, :, :],
             )
         def load_rest():
+            load_w1s(*S_LOADS[1])
             nc.sync.dma_start(out=w2[:].bitcast(I32), in_=w2_words.rearrange("e s p b -> p (e s) b").bitcast(I32))
 
         w2 = keep.tile([P, E, 2 * N], U8, align_bytes=64, name="w2")
@@ -133,7 +142,7 @@ def tile_moe_tk_mlp_relu_kernel(tc, xT, w1_words, w1_scales, w2_words, w2_scales
                         in_=gs[32 * q + 4 : 32 * q + 8, lo:b].bitcast(I32),
                     )
 
-        for s, engines in ((0, "vsv"), (1, "svs")):
+        for s, engines in ((0, "vsv"), (1, "sss")):
             xbs = [interleave(s, i, engines[i]) for i in range(3)]
             for i in range(3):
                 quantise_x(s, i, xbs[i])
@@ -142,11 +151,11 @@ def tile_moe_tk_mlp_relu_kernel(tc, xT, w1_words, w1_scales, w2_words, w2_scales
         gather_scales(0)
         gather_words(1, 0)
         load_rest()
-        load_w1(*W_LOADS[1])
+        for a, b in W_LOADS[1:]:
+            load_w1(a, b)
         gather_scales(1)
         gather_scales(2)
         gather_words(0, 1)
-        load_w1(*W_LOADS[2])
         gather_words(1, 1)
         scaled = 3
 
@@ -160,13 +169,14 @@ def tile_moe_tk_mlp_relu_kernel(tc, xT, w1_words, w1_scales, w2_words, w2_scales
                 w, at = w1[e]
                 slots = slice(e * C, (e + 1) * C)
                 for s in range(PASSES):
-                    cols = slice((e * PASSES + s) * H, (e * PASSES + s + 1) * H)
+                    first = max(l[0] for l in S_LOADS if l[0] <= e)
+                    cols = slice(((e - first) * PASSES + s) * H, ((e - first) * PASSES + s + 1) * H)
                     nc.tensor.matmul_mx(
                         out=acc[:],
                         lhsT=gw[s][:, slots].bitcast(FP8X4),
                         lhsT_scale=(gs, gs1)[s][:, slots],
                         rhs=w[:, at, s, :].bitcast(FP4X4),
-                        rhs_scale=w1s[:, cols],
+                        rhs_scale=w1s[first][:, cols],
                         start=(s == 0),
                         stop=(s == PASSES - 1),
                     )
@@ -199,7 +209,6 @@ def tile_moe_tk_mlp_relu_kernel(tc, xT, w1_words, w1_scales, w2_words, w2_scales
             nc.scalar.copy(out=y_all[:, a * C : b * C], in_=y[:])
 
         gathered = 2
-        loaded = 3
         for a, b in GROUPS:
             while gathered < len(CHUNKS) and CHUNKS[gathered - 1][0] <= b:
                 while scaled < len(CHUNKS) and scaled <= gathered + 3:
@@ -208,11 +217,8 @@ def tile_moe_tk_mlp_relu_kernel(tc, xT, w1_words, w1_scales, w2_words, w2_scales
                 gather_words(0, gathered)
                 gather_words(1, gathered)
                 gathered += 1
-            if loaded < len(W_LOADS) and W_LOADS[loaded - 2][0] <= a:
-                load_w1(*W_LOADS[loaded])
-                loaded += 1
             if a == 10:
-                gates = wring.tile([P, TOP, T], F32, align_bytes=64, tag="w1", name="gates")
+                gates = wring.tile([P, TOP, T], F32, align_bytes=64, tag="big", name="gates")
                 nc.sync.dma_start(out=gates[:], in_=gate.rearrange("r n t -> n r t"))
             experts(a, b)
 

@@ -22,12 +22,12 @@ S = E * C
 PASSES = K // 512
 FLOPS = 2 * S * H * (K + N)
 
-CHUNKS = ((0, 2), (2, 5), (5, 8), (8, 11), (11, 14), (14, 15))
-W_LOADS = ((0, 2), (2, 5), (5, 8), (8, 11), (11, 15))
-SHIFTS = {0: (0, 2), 2: (2, 8), 5: (8, 15)}
-GROUPS = ((0, 2), (2, 4), (4, 6), (6, 8), (8, 10), (10, 12), (12, 14), (14, 15))
-VECTOR_TURNS = (4, 8, 12)
-S_LOADS = ((0, 5), (5, 15))
+CHUNKS = ((0, 1), (1, 3), (3, 6), (6, 9), (9, 12), (12, 15))
+W_LOADS = ((0, 2), (2, 4), (4, 6), (6, 8), (8, 10), (10, 12), (12, 15))
+SHIFTS = {0: (0, 1), 1: (1, 3), 2: (3, 6), 5: (6, 15)}
+GROUPS = ((0, 1), (1, 3), (3, 5), (5, 7), (7, 9), (9, 11), (11, 13), (13, 14), (14, 15))
+VECTOR_TURNS = ()
+S_LOADS = ((0, 9), (9, 15))
 T_LOADS = ((0, 256), (256, 640))
 T_PARTS = ((0, 256), (256, 512), (512, 640))
 
@@ -37,7 +37,8 @@ def tile_moe_tk_mlp_relu_kernel(tc, xT, w1_words, w1_scales, w2_words, w2_scales
     with ExitStack() as ctx:
         lists = ctx.enter_context(tc.tile_pool(name="lists", bufs=1))
         keep = ctx.enter_context(tc.tile_pool(name="keep", bufs=1))
-        wring = ctx.enter_context(tc.tile_pool(name="wring", bufs=4))
+        wring = ctx.enter_context(tc.tile_pool(name="wring", bufs=3))
+        gring = ctx.enter_context(tc.tile_pool(name="gring", bufs=3))
         ring = ctx.enter_context(tc.tile_pool(name="ring", bufs=4))
         psum_a = ctx.enter_context(tc.psum_pool(name="psum_a", bufs=4))
         psum_t = ctx.enter_context(tc.psum_pool(name="psum_t", bufs=2))
@@ -52,14 +53,14 @@ def tile_moe_tk_mlp_relu_kernel(tc, xT, w1_words, w1_scales, w2_words, w2_scales
         w2s = keep.tile([P, E * N], U8, align_bytes=64, name="w2s")
         xs = keep.tile([P, T], U8, align_bytes=64, name="xs")
         gs1 = keep.tile([P, S], U8, align_bytes=64, name="gs1")
-        for t in (w1s[0], w1s[S_LOADS[1][0]], xs, w2s, gs1):
+        for t in (w1s[0], w2s, w1s[S_LOADS[1][0]], xs, gs1):
             nc.vector.memset(t[:].bitcast(I32), 0)
 
         w1s_view = w1_scales.rearrange("e s q i -> q (e s) i").bitcast(I32)
 
-        def load_w1s(a, b):
+        def load_w1s(a, b, queue):
             for q in range(4):
-                nc.sync.dma_start(
+                queue.dma_start(
                     out=w1s[a][32 * q : 32 * q + 4, :].bitcast(I32).rearrange("q (a i) -> q a i", i=H // 4),
                     in_=w1s_view[4 * q : 4 * q + 4, a * PASSES : b * PASSES, :],
                 )
@@ -68,43 +69,41 @@ def tile_moe_tk_mlp_relu_kernel(tc, xT, w1_words, w1_scales, w2_words, w2_scales
         x_raw = {}
         for s in range(PASSES):
             for a, b in T_LOADS:
-                raw = wring.tile([P, 4, b - a], F32, align_bytes=64, tag="big", name="x_raw_%d_%d" % (s, a))
+                raw = keep.tile([P, 4, b - a], F32, name="x_raw_%d_%d" % (s, a))
                 nc.sync.dma_start(out=raw[:], in_=x_view[s, :, :, a:b])
                 x_raw[s, a] = raw
             if s == 0:
                 nc.sync.dma_start(offs_t[:], offs)
+                load_w1s(*S_LOADS[0], nc.sync)
 
         w1 = {}
         w1_view = w1_words.rearrange("e s p b -> p e s b").bitcast(I32)
         w2s_view = w2_scales.rearrange("e s q n -> q (e s) n").bitcast(I32)
         def load_w1(a, b):
-            if a == 0:
-                w = keep.tile([P, b - a, PASSES, 2 * H], U8, align_bytes=64, name="w1_first")
-            else:
-                w = wring.tile([P, 4, PASSES, 2 * H], U8, align_bytes=64, tag="big", name="w1")
+            w = wring.tile([P, 3, PASSES, 2 * H], U8, align_bytes=64, tag="big", name="w1")
             nc.sync.dma_start(out=w[:, : b - a].bitcast(I32), in_=w1_view[:, a:b])
             for e in range(a, b):
                 w1[e] = (w, e - a)
 
         load_w1(*W_LOADS[0])
-        load_w1s(*S_LOADS[0])
         for r, pos in enumerate((pos1, pos2, pos3)):
             nc.sync.dma_start(pos_t[r][:], pos)
         ident = keep.tile([P, P], F32, name="ident")
         make_identity(nc, ident[:])
         for q in range(4):
-            nc.sync.dma_start(
+            nc.gpsimd.dma_start(
                 out=w2s[32 * q : 32 * q + 4, :].bitcast(I32).rearrange("q (a n) -> q a n", n=N // 4),
                 in_=w2s_view[4 * q : 4 * q + 4, :, :],
             )
+        load_w1s(*S_LOADS[1], nc.gpsimd)
+
         def load_rest():
-            load_w1s(*S_LOADS[1])
             nc.sync.dma_start(out=w2[:].bitcast(I32), in_=w2_words.rearrange("e s p b -> p (e s) b").bitcast(I32))
 
         w2 = keep.tile([P, E, 2 * N], U8, align_bytes=64, name="w2")
 
         xw = [keep.tile([P, T], U32, align_bytes=64, name="xw%d" % s) for s in range(PASSES)]
-        gw = [keep.tile([P, S], U32, align_bytes=64, name="gw%d" % s) for s in range(PASSES)]
+        gw = {}
         gs = keep.tile([P, S], U8, align_bytes=64, name="gs")
 
         def interleave(s, i, engine):
@@ -129,35 +128,33 @@ def tile_moe_tk_mlp_relu_kernel(tc, xT, w1_words, w1_scales, w2_words, w2_scales
 
         def gather_words(s, c):
             a, b = CHUNKS[c][0] * C, CHUNKS[c][1] * C
-            nc.vector.tensor_copy(out=gw[s][:, a:b], in_=xw[s][:].indirect(offs_t[:, a // 16 : b // 16]))
+            words = gring.tile([P, 3 * C], U32, align_bytes=64, tag="gw%d" % s, name="words")
+            nc.vector.tensor_copy(out=words[:, : b - a], in_=xw[s][:].indirect(offs_t[:, a // 16 : b // 16]))
+            for e in range(*CHUNKS[c]):
+                gw[s, e] = words[:, e * C - a : (e + 1) * C - a]
 
         def gather_scales(c):
             a, b = CHUNKS[c][0] * C, CHUNKS[c][1] * C
             nc.vector.tensor_copy(out=gs[:, a:b], in_=xs[:].indirect(offs_t[:, a // 16 : b // 16]))
             if CHUNKS[c][1] in [x[1] for x in SHIFTS.values()]:
                 lo = [x for x in SHIFTS.values() if x[1] == CHUNKS[c][1]][0][0] * C
-                for q in range(4):
-                    nc.scalar.dma_start(
-                        out=gs1[32 * q : 32 * q + 4, lo:b].bitcast(I32),
-                        in_=gs[32 * q + 4 : 32 * q + 8, lo:b].bitcast(I32),
-                    )
+                nc.scalar.dma_start(out=gs1[0:112, lo:b].bitcast(I32), in_=gs[4:116, lo:b].bitcast(I32))
 
-        for s, engines in ((0, "vsv"), (1, "sss")):
+        for s, engines in ((0, "vsv"), (1, "svv")):
             xbs = [interleave(s, i, engines[i]) for i in range(3)]
             for i in range(3):
                 quantise_x(s, i, xbs[i])
             if s == 0:
                 gather_words(0, 0)
+                gather_words(0, 1)
         gather_scales(0)
         gather_words(1, 0)
         load_rest()
-        for a, b in W_LOADS[1:]:
+        for a, b in W_LOADS[1:3]:
             load_w1(a, b)
         gather_scales(1)
-        gather_scales(2)
-        gather_words(0, 1)
         gather_words(1, 1)
-        scaled = 3
+        gather_scales(2)
 
         y_all = keep.tile([P, S], F32, name="y_all")
 
@@ -173,7 +170,7 @@ def tile_moe_tk_mlp_relu_kernel(tc, xT, w1_words, w1_scales, w2_words, w2_scales
                     cols = slice(((e - first) * PASSES + s) * H, ((e - first) * PASSES + s + 1) * H)
                     nc.tensor.matmul_mx(
                         out=acc[:],
-                        lhsT=gw[s][:, slots].bitcast(FP8X4),
+                        lhsT=gw[s, e].bitcast(FP8X4),
                         lhsT_scale=(gs, gs1)[s][:, slots],
                         rhs=w[:, at, s, :].bitcast(FP4X4),
                         rhs_scale=w1s[first][:, cols],
@@ -209,15 +206,19 @@ def tile_moe_tk_mlp_relu_kernel(tc, xT, w1_words, w1_scales, w2_words, w2_scales
             nc.scalar.copy(out=y_all[:, a * C : b * C], in_=y[:])
 
         gathered = 2
+        loaded = 3
         for a, b in GROUPS:
-            while gathered < len(CHUNKS) and CHUNKS[gathered - 1][0] <= b:
-                while scaled < len(CHUNKS) and scaled <= gathered + 3:
-                    gather_scales(scaled)
-                    scaled += 1
+            while gathered < len(CHUNKS) and (gathered < 3 or CHUNKS[gathered - 3][1] <= a):
+                if gathered == 3:
+                    for c in range(3, len(CHUNKS)):
+                        gather_scales(c)
                 gather_words(0, gathered)
                 gather_words(1, gathered)
                 gathered += 1
-            if a == 10:
+            while loaded < len(W_LOADS) and W_LOADS[loaded - 3][1] <= a:
+                load_w1(*W_LOADS[loaded])
+                loaded += 1
+            if a == 11:
                 gates = wring.tile([P, TOP, T], F32, align_bytes=64, tag="big", name="gates")
                 nc.sync.dma_start(out=gates[:], in_=gate.rearrange("r n t -> n r t"))
             experts(a, b)

@@ -23,10 +23,11 @@ PASSES = K // 512
 FLOPS = 2 * S * H * (K + N)
 
 CHUNKS = ((0, 1), (1, 3), (3, 6), (6, 9), (9, 12), (12, 15))
-W_LOADS = ((0, 2), (2, 4), (4, 6), (6, 8), (8, 10), (10, 12), (12, 15))
-SHIFTS = {0: (0, 1), 1: (1, 3), 2: (3, 6), 5: (6, 15)}
-GROUPS = ((0, 1), (1, 3), (3, 5), (5, 7), (7, 9), (9, 11), (11, 13), (13, 14), (14, 15))
-VECTOR_TURNS = ()
+W_LOADS = ((0, 2), (2, 5), (5, 8), (8, 11), (11, 15))
+SHIFTS = {0: (0, 1), 2: (1, 6), 5: (6, 15)}
+BATCHES = ((0, 4), (4, 8), (8, 12), (12, 14), (14, 15))
+VECTOR_TURNS = (8, 10, 12, 14)
+OUT_PARTS = ((0, 512), (512, 640))
 S_LOADS = ((0, 9), (9, 15))
 T_LOADS = ((0, 256), (256, 640))
 T_PARTS = ((0, 256), (256, 512), (512, 640))
@@ -37,12 +38,11 @@ def tile_moe_tk_mlp_relu_kernel(tc, xT, w1_words, w1_scales, w2_words, w2_scales
     with ExitStack() as ctx:
         lists = ctx.enter_context(tc.tile_pool(name="lists", bufs=1))
         keep = ctx.enter_context(tc.tile_pool(name="keep", bufs=1))
-        wring = ctx.enter_context(tc.tile_pool(name="wring", bufs=3))
-        gring = ctx.enter_context(tc.tile_pool(name="gring", bufs=3))
+        gring = ctx.enter_context(tc.tile_pool(name="gring", bufs=4))
         ring = ctx.enter_context(tc.tile_pool(name="ring", bufs=4))
-        psum_a = ctx.enter_context(tc.psum_pool(name="psum_a", bufs=4))
+        psum_a = ctx.enter_context(tc.psum_pool(name="psum_a", bufs=5))
         psum_t = ctx.enter_context(tc.psum_pool(name="psum_t", bufs=2))
-        psum_y = ctx.enter_context(tc.psum_pool(name="psum_y", bufs=2))
+        psum_y = ctx.enter_context(tc.psum_pool(name="psum_y", bufs=1))
 
         offs_t = lists.tile([P, S // 16], U16, name="offs_t")
         pos_t = [lists.tile([P, T // 16], U16, name="pos_t%d" % r) for r in range(TOP)]
@@ -80,8 +80,8 @@ def tile_moe_tk_mlp_relu_kernel(tc, xT, w1_words, w1_scales, w2_words, w2_scales
         w1_view = w1_words.rearrange("e s p b -> p e s b").bitcast(I32)
         w2s_view = w2_scales.rearrange("e s q n -> q (e s) n").bitcast(I32)
         def load_w1(a, b):
-            w = wring.tile([P, 3, PASSES, 2 * H], U8, align_bytes=64, tag="big", name="w1")
-            nc.sync.dma_start(out=w[:, : b - a].bitcast(I32), in_=w1_view[:, a:b])
+            w = keep.tile([P, b - a, PASSES, 2 * H], U8, align_bytes=64, name="w1_%d" % a)
+            nc.sync.dma_start(out=w[:].bitcast(I32), in_=w1_view[:, a:b])
             for e in range(a, b):
                 w1[e] = (w, e - a)
 
@@ -128,7 +128,10 @@ def tile_moe_tk_mlp_relu_kernel(tc, xT, w1_words, w1_scales, w2_words, w2_scales
 
         def gather_words(s, c):
             a, b = CHUNKS[c][0] * C, CHUNKS[c][1] * C
-            words = gring.tile([P, 3 * C], U32, align_bytes=64, tag="gw%d" % s, name="words")
+            if s == 0:
+                words = gring.tile([P, 3 * C], U32, align_bytes=64, name="words")
+            else:
+                words = keep.tile([P, b - a], U32, align_bytes=64, name="words1_%d" % c)
             nc.vector.tensor_copy(out=words[:, : b - a], in_=xw[s][:].indirect(offs_t[:, a // 16 : b // 16]))
             for e in range(*CHUNKS[c]):
                 gw[s, e] = words[:, e * C - a : (e + 1) * C - a]
@@ -140,6 +143,12 @@ def tile_moe_tk_mlp_relu_kernel(tc, xT, w1_words, w1_scales, w2_words, w2_scales
                 lo = [x for x in SHIFTS.values() if x[1] == CHUNKS[c][1]][0][0] * C
                 nc.scalar.dma_start(out=gs1[0:112, lo:b].bitcast(I32), in_=gs[4:116, lo:b].bitcast(I32))
 
+        load_rest()
+        for a, b in W_LOADS[1:]:
+            load_w1(a, b)
+        gates = keep.tile([P, TOP, T], F32, name="gates")
+        nc.sync.dma_start(out=gates[:], in_=gate.rearrange("r n t -> n r t"))
+
         for s, engines in ((0, "vsv"), (1, "svv")):
             xbs = [interleave(s, i, engines[i]) for i in range(3)]
             for i in range(3):
@@ -149,47 +158,55 @@ def tile_moe_tk_mlp_relu_kernel(tc, xT, w1_words, w1_scales, w2_words, w2_scales
                 gather_words(0, 1)
         gather_scales(0)
         gather_words(1, 0)
-        load_rest()
-        for a, b in W_LOADS[1:3]:
-            load_w1(a, b)
         gather_scales(1)
-        gather_words(1, 1)
         gather_scales(2)
+        gather_words(1, 1)
+        gather_words(0, 2)
+        gather_words(1, 2)
+        gather_words(0, 3)
+        for c in range(3, len(CHUNKS)):
+            gather_scales(c)
+        gather_words(1, 3)
 
         y_all = keep.tile([P, S], F32, name="y_all")
 
-        def experts(a, b):
+        def first_layer(e):
+            acc = psum_a.tile([C, H], F32, name="acc")
+            w, at = w1[e]
+            slots = slice(e * C, (e + 1) * C)
+            first = max(l[0] for l in S_LOADS if l[0] <= e)
+            for s in range(PASSES):
+                cols = slice(((e - first) * PASSES + s) * H, ((e - first) * PASSES + s + 1) * H)
+                nc.tensor.matmul_mx(
+                    out=acc[:],
+                    lhsT=gw[s, e].bitcast(FP8X4),
+                    lhsT_scale=(gs, gs1)[s][:, slots],
+                    rhs=w[:, at, s, :].bitcast(FP4X4),
+                    rhs_scale=w1s[first][:, cols],
+                    start=(s == 0),
+                    stop=(s == PASSES - 1),
+                )
+            h = ring.tile([C, 2, P, 2], BF16, name="h")
+            nc.scalar.activation(out=h[:], in_=acc[:].rearrange("c (p u d) -> c u p d", u=2, d=2), func=ACT.Relu)
+            return h[:].rearrange("c u p d -> c (u p d)").bitcast(F32)
+
+        def turn(a, b, hb):
             n = b - a
             ht = psum_t.tile([P, n, 2, C], F32, name="ht")
             for e in range(a, b):
-                acc = psum_a.tile([C, H], F32, name="acc")
-                w, at = w1[e]
-                slots = slice(e * C, (e + 1) * C)
-                for s in range(PASSES):
-                    first = max(l[0] for l in S_LOADS if l[0] <= e)
-                    cols = slice(((e - first) * PASSES + s) * H, ((e - first) * PASSES + s + 1) * H)
-                    nc.tensor.matmul_mx(
-                        out=acc[:],
-                        lhsT=gw[s, e].bitcast(FP8X4),
-                        lhsT_scale=(gs, gs1)[s][:, slots],
-                        rhs=w[:, at, s, :].bitcast(FP4X4),
-                        rhs_scale=w1s[first][:, cols],
-                        start=(s == 0),
-                        stop=(s == PASSES - 1),
-                    )
-                h = ring.tile([C, 2, P, 2], BF16, name="h")
-                nc.scalar.activation(out=h[:], in_=acc[:].rearrange("c (p u d) -> c u p d", u=2, d=2), func=ACT.Relu)
-                pairs = h[:].rearrange("c u p d -> c (u p d)").bitcast(F32)
+                pairs = first_layer(e)
                 for u in range(2):
                     nc.tensor.transpose(ht[:, e - a, u, :], pairs[:, u * P : (u + 1) * P], ident[:])
-            hb = ring.tile([P, n * C, 4], BF16, align_bytes=64, name="hb")
             copy = nc.vector.tensor_copy if a in VECTOR_TURNS else nc.scalar.copy
             copy(
-                out=hb[:].rearrange("p c d -> p (c d)").bitcast(F32).rearrange("p (g c u) -> p g c u", g=n, u=2),
+                out=hb.rearrange("p c d -> p (c d)").bitcast(F32).rearrange("p (g c u) -> p g c u", g=n, u=2),
                 in_=ht[:].rearrange("p g u c -> p g c u"),
             )
-            hw = ring.tile([P, n * C], U32, align_bytes=64, name="hw")
-            hs = ring.tile([P, n * C], U8, align_bytes=64, name="hs")
+
+        def second_layer(a, b, hb):
+            n = b - a
+            hw = keep.tile([P, n * C], U32, align_bytes=64, name="hw_%d" % a)
+            hs = keep.tile([P, n * C], U8, align_bytes=64, name="hs_%d" % a)
             nc.vector.quantize_mx(out=hw[:].bitcast(FP8X4), scales=hs[:], in_=hb[:].rearrange("p c d -> p (c d)"))
             y = psum_y.tile([N, n * C], F32, name="y")
             for e in range(a, b):
@@ -205,39 +222,31 @@ def tile_moe_tk_mlp_relu_kernel(tc, xT, w1_words, w1_scales, w2_words, w2_scales
                 )
             nc.scalar.copy(out=y_all[:, a * C : b * C], in_=y[:])
 
-        gathered = 2
-        loaded = 3
-        for a, b in GROUPS:
-            while gathered < len(CHUNKS) and (gathered < 3 or CHUNKS[gathered - 3][1] <= a):
-                if gathered == 3:
-                    for c in range(3, len(CHUNKS)):
-                        gather_scales(c)
-                gather_words(0, gathered)
-                gather_words(1, gathered)
-                gathered += 1
-            while loaded < len(W_LOADS) and W_LOADS[loaded - 3][1] <= a:
-                load_w1(*W_LOADS[loaded])
-                loaded += 1
-            if a == 11:
-                gates = wring.tile([P, TOP, T], F32, align_bytes=64, tag="big", name="gates")
-                nc.sync.dma_start(out=gates[:], in_=gate.rearrange("r n t -> n r t"))
-            experts(a, b)
+        gathered = 4
+        for i, (a, b) in enumerate(BATCHES):
+            hb = keep.tile([P, (b - a) * C, 4], BF16, align_bytes=64, name="hb_%d" % a)
+            for e in range(a, b, 2):
+                f = min(e + 2, b)
+                while gathered < len(CHUNKS) and CHUNKS[gathered - 4][1] <= e:
+                    gather_words(0, gathered)
+                    gather_words(1, gathered)
+                    gathered += 1
+                turn(e, f, hb[:, (e - a) * C : (f - a) * C, :])
+            second_layer(a, b, hb)
 
-        half = T // 2
-        for i in range(2):
-            t = slice(i * half, (i + 1) * half)
+        for a, b in OUT_PARTS:
             prods = []
             for r in range(TOP):
-                prod = keep.tile([N, half], F32, name="prod_%d_%d" % (i, r))
+                prod = keep.tile([N, b - a], F32, name="prod_%d_%d" % (a, r))
                 nc.vector.tensor_tensor(
                     out=prod[:],
-                    in0=y_all[:].indirect(pos_t[r][:, i * half // 16 : (i + 1) * half // 16]),
-                    in1=gates[:, r, t],
+                    in0=y_all[:].indirect(pos_t[r][:, a // 16 : b // 16]),
+                    in1=gates[:, r, a:b],
                     op=MULT,
                 )
                 prods.append(prod)
-            part = keep.tile([N, half], F32, name="part_%d" % i)
+            part = keep.tile([N, b - a], F32, name="part_%d" % a)
             nc.vector.tensor_tensor(out=part[:], in0=prods[0][:], in1=prods[1][:], op=ADD)
-            result = keep.tile([N, half], F32, name="result_%d" % i)
+            result = keep.tile([N, b - a], F32, name="result_%d" % a)
             nc.vector.tensor_tensor(out=result[:], in0=part[:], in1=prods[2][:], op=ADD)
-            nc.sync.dma_start(out=out[:, t], in_=result[:])
+            nc.sync.dma_start(out=out[:, a:b], in_=result[:])

@@ -24,12 +24,11 @@ FLOPS = 2 * S * H * (K + N)
 
 CHUNKS = ((0, 1), (1, 3), (3, 6), (6, 9), (9, 12), (12, 15))
 W_LOADS = ((0, 2), (2, 5), (5, 8), (8, 11), (11, 15))
-SHIFTS = {0: (0, 1), 2: (1, 6), 5: (6, 15)}
+SHIFTS = {0: (0, 1), 2: (1, 6), 3: (6, 9), 5: (9, 15)}
 BATCHES = ((0, 4), (4, 8), (8, 12), (12, 14), (14, 15))
-VECTOR_TURNS = (8, 10, 12, 14)
+VECTOR_TURNS = (10, 12, 14)
 OUT_PARTS = ((0, 512), (512, 640))
-S_LOADS = ((0, 9), (9, 15))
-T_LOADS = ((0, 256), (256, 640))
+T_LOADS = ((0, 640),)
 T_PARTS = ((0, 256), (256, 512), (512, 640))
 
 
@@ -47,23 +46,22 @@ def tile_moe_tk_mlp_relu_kernel(tc, xT, w1_words, w1_scales, w2_words, w2_scales
         offs_t = lists.tile([P, S // 16], U16, name="offs_t")
         pos_t = [lists.tile([P, T // 16], U16, name="pos_t%d" % r) for r in range(TOP)]
 
-        w1s = {}
-        for a, b in S_LOADS:
-            w1s[a] = keep.tile([P, (b - a) * PASSES * H], U8, align_bytes=64, name="w1s_%d" % a)
+        w1s = keep.tile([P, E * PASSES * H], U8, align_bytes=64, name="w1s")
         w2s = keep.tile([P, E * N], U8, align_bytes=64, name="w2s")
         xs = keep.tile([P, T], U8, align_bytes=64, name="xs")
         gs1 = keep.tile([P, S], U8, align_bytes=64, name="gs1")
-        for t in (w1s[0], w2s, w1s[S_LOADS[1][0]], xs, gs1):
+        for t in (w2s, w1s, xs, gs1):
             nc.vector.memset(t[:].bitcast(I32), 0)
 
         w1s_view = w1_scales.rearrange("e s q i -> q (e s) i").bitcast(I32)
-
-        def load_w1s(a, b, queue):
-            for q in range(4):
-                queue.dma_start(
-                    out=w1s[a][32 * q : 32 * q + 4, :].bitcast(I32).rearrange("q (a i) -> q a i", i=H // 4),
-                    in_=w1s_view[4 * q : 4 * q + 4, a * PASSES : b * PASSES, :],
-                )
+        w2s_view = w2_scales.rearrange("e s q n -> q (e s) n").bitcast(I32)
+        for q in range(4):
+            nc.gpsimd.dma_start(
+                out=w2s[32 * q : 32 * q + 4, :].bitcast(I32).rearrange("q (a n) -> q a n", n=N // 4),
+                in_=w2s_view[4 * q : 4 * q + 4, :, :],
+            )
+        ident = keep.tile([P, P], F32, name="ident")
+        make_identity(nc, ident[:])
 
         x_view = xT.rearrange("(s p j) t -> s p j t", p=P, j=4)
         x_raw = {}
@@ -74,11 +72,12 @@ def tile_moe_tk_mlp_relu_kernel(tc, xT, w1_words, w1_scales, w2_words, w2_scales
                 x_raw[s, a] = raw
             if s == 0:
                 nc.sync.dma_start(offs_t[:], offs)
-                load_w1s(*S_LOADS[0], nc.sync)
+                for r, pos in enumerate((pos1, pos2, pos3)):
+                    nc.sync.dma_start(pos_t[r][:], pos)
 
         w1 = {}
         w1_view = w1_words.rearrange("e s p b -> p e s b").bitcast(I32)
-        w2s_view = w2_scales.rearrange("e s q n -> q (e s) n").bitcast(I32)
+
         def load_w1(a, b):
             w = keep.tile([P, b - a, PASSES, 2 * H], U8, align_bytes=64, name="w1_%d" % a)
             nc.sync.dma_start(out=w[:].bitcast(I32), in_=w1_view[:, a:b])
@@ -86,16 +85,11 @@ def tile_moe_tk_mlp_relu_kernel(tc, xT, w1_words, w1_scales, w2_words, w2_scales
                 w1[e] = (w, e - a)
 
         load_w1(*W_LOADS[0])
-        for r, pos in enumerate((pos1, pos2, pos3)):
-            nc.sync.dma_start(pos_t[r][:], pos)
-        ident = keep.tile([P, P], F32, name="ident")
-        make_identity(nc, ident[:])
         for q in range(4):
-            nc.gpsimd.dma_start(
-                out=w2s[32 * q : 32 * q + 4, :].bitcast(I32).rearrange("q (a n) -> q a n", n=N // 4),
-                in_=w2s_view[4 * q : 4 * q + 4, :, :],
+            nc.sync.dma_start(
+                out=w1s[32 * q : 32 * q + 4, :].bitcast(I32).rearrange("q (a i) -> q a i", i=H // 4),
+                in_=w1s_view[4 * q : 4 * q + 4, :, :],
             )
-        load_w1s(*S_LOADS[1], nc.gpsimd)
 
         def load_rest():
             nc.sync.dma_start(out=w2[:].bitcast(I32), in_=w2_words.rearrange("e s p b -> p (e s) b").bitcast(I32))
@@ -149,7 +143,7 @@ def tile_moe_tk_mlp_relu_kernel(tc, xT, w1_words, w1_scales, w2_words, w2_scales
         gates = keep.tile([P, TOP, T], F32, name="gates")
         nc.sync.dma_start(out=gates[:], in_=gate.rearrange("r n t -> n r t"))
 
-        for s, engines in ((0, "vsv"), (1, "svv")):
+        for s, engines in ((0, "svv"), (1, "svv")):
             xbs = [interleave(s, i, engines[i]) for i in range(3)]
             for i in range(3):
                 quantise_x(s, i, xbs[i])
@@ -164,9 +158,10 @@ def tile_moe_tk_mlp_relu_kernel(tc, xT, w1_words, w1_scales, w2_words, w2_scales
         gather_words(0, 2)
         gather_words(1, 2)
         gather_words(0, 3)
-        for c in range(3, len(CHUNKS)):
-            gather_scales(c)
+        gather_scales(3)
         gather_words(1, 3)
+        gather_scales(4)
+        gather_scales(5)
 
         y_all = keep.tile([P, S], F32, name="y_all")
 
@@ -174,15 +169,14 @@ def tile_moe_tk_mlp_relu_kernel(tc, xT, w1_words, w1_scales, w2_words, w2_scales
             acc = psum_a.tile([C, H], F32, name="acc")
             w, at = w1[e]
             slots = slice(e * C, (e + 1) * C)
-            first = max(l[0] for l in S_LOADS if l[0] <= e)
             for s in range(PASSES):
-                cols = slice(((e - first) * PASSES + s) * H, ((e - first) * PASSES + s + 1) * H)
+                cols = slice((e * PASSES + s) * H, (e * PASSES + s + 1) * H)
                 nc.tensor.matmul_mx(
                     out=acc[:],
                     lhsT=gw[s, e].bitcast(FP8X4),
                     lhsT_scale=(gs, gs1)[s][:, slots],
                     rhs=w[:, at, s, :].bitcast(FP4X4),
-                    rhs_scale=w1s[first][:, cols],
+                    rhs_scale=w1s[:, cols],
                     start=(s == 0),
                     stop=(s == PASSES - 1),
                 )

from contextlib import ExitStack

import concourse.mybir as mybir
from concourse.masks import make_identity

F32 = mybir.dt.float32
BF16 = mybir.dt.bfloat16
I32 = mybir.dt.int32
U32 = mybir.dt.uint32
U16 = mybir.dt.uint16
U8 = mybir.dt.uint8
FP8X4 = mybir.dt.float8_e4m3fn_x4
FP4X4 = mybir.dt.float4_e2m1fn_x4
ACT = mybir.ActivationFunctionType
MULT = mybir.AluOpType.mult
ADD = mybir.AluOpType.add

P = 128
K, T, E, C, H, N = 1024, 640, 15, 128, 512, 128
TOP = 3
S = E * C
PASSES = K // 512
FLOPS = 2 * S * H * (K + N)

CHUNKS = ((0, 1), (1, 3), (3, 6), (6, 9), (9, 12), (12, 15))
W_LOADS = ((0, 2), (2, 5), (5, 8), (8, 11), (11, 15))
SHIFTS = {0: (0, 1), 2: (1, 6), 3: (6, 9), 5: (9, 15)}
BATCHES = ((0, 4), (4, 8), (8, 12), (12, 14), (14, 15))
VECTOR_TURNS = (10, 12, 14)
OUT_PARTS = ((0, 512), (512, 640))
T_LOADS = ((0, 640),)
T_PARTS = ((0, 256), (256, 512), (512, 640))


def tile_moe_tk_mlp_relu_kernel(tc, xT, w1_words, w1_scales, w2_words, w2_scales, gate, offs, pos1, pos2, pos3, out):
    nc = tc.nc
    with ExitStack() as ctx:
        lists = ctx.enter_context(tc.tile_pool(name="lists", bufs=1))
        keep = ctx.enter_context(tc.tile_pool(name="keep", bufs=1))
        gring = ctx.enter_context(tc.tile_pool(name="gring", bufs=4))
        ring = ctx.enter_context(tc.tile_pool(name="ring", bufs=4))
        psum_a = ctx.enter_context(tc.psum_pool(name="psum_a", bufs=5))
        psum_t = ctx.enter_context(tc.psum_pool(name="psum_t", bufs=2))
        psum_y = ctx.enter_context(tc.psum_pool(name="psum_y", bufs=1))

        offs_t = lists.tile([P, S // 16], U16, name="offs_t")
        pos_t = [lists.tile([P, T // 16], U16, name="pos_t%d" % r) for r in range(TOP)]

        w1s = keep.tile([P, E * PASSES * H], U8, align_bytes=64, name="w1s")
        w2s = keep.tile([P, E * N], U8, align_bytes=64, name="w2s")
        xs = keep.tile([P, T], U8, align_bytes=64, name="xs")
        gs1 = keep.tile([P, S], U8, align_bytes=64, name="gs1")
        for t in (w2s, w1s, xs, gs1):
            nc.vector.memset(t[:].bitcast(I32), 0)

        w1s_view = w1_scales.rearrange("e s q i -> q (e s) i").bitcast(I32)
        w2s_view = w2_scales.rearrange("e s q n -> q (e s) n").bitcast(I32)
        for q in range(4):
            nc.gpsimd.dma_start(
                out=w2s[32 * q : 32 * q + 4, :].bitcast(I32).rearrange("q (a n) -> q a n", n=N // 4),
                in_=w2s_view[4 * q : 4 * q + 4, :, :],
            )
        ident = keep.tile([P, P], F32, name="ident")
        make_identity(nc, ident[:])

        x_view = xT.rearrange("(s p j) t -> s p j t", p=P, j=4)
        x_raw = {}
        for s in range(PASSES):
            for a, b in T_LOADS:
                raw = keep.tile([P, 4, b - a], F32, name="x_raw_%d_%d" % (s, a))
                nc.sync.dma_start(out=raw[:], in_=x_view[s, :, :, a:b])
                x_raw[s, a] = raw
            if s == 0:
                nc.sync.dma_start(offs_t[:], offs)
                for r, pos in enumerate((pos1, pos2, pos3)):
                    nc.sync.dma_start(pos_t[r][:], pos)

        w1 = {}
        w1_view = w1_words.rearrange("e s p b -> p e s b").bitcast(I32)

        def load_w1(a, b):
            w = keep.tile([P, b - a, PASSES, 2 * H], U8, align_bytes=64, name="w1_%d" % a)
            nc.sync.dma_start(out=w[:].bitcast(I32), in_=w1_view[:, a:b])
            for e in range(a, b):
                w1[e] = (w, e - a)

        load_w1(*W_LOADS[0])
        for q in range(4):
            nc.sync.dma_start(
                out=w1s[32 * q : 32 * q + 4, :].bitcast(I32).rearrange("q (a i) -> q a i", i=H // 4),
                in_=w1s_view[4 * q : 4 * q + 4, :, :],
            )

        def load_rest():
            nc.sync.dma_start(out=w2[:].bitcast(I32), in_=w2_words.rearrange("e s p b -> p (e s) b").bitcast(I32))

        w2 = keep.tile([P, E, 2 * N], U8, align_bytes=64, name="w2")

        xw = [keep.tile([P, T], U32, align_bytes=64, name="xw%d" % s) for s in range(PASSES)]
        gw = {}
        gs = keep.tile([P, S], U8, align_bytes=64, name="gs")

        def interleave(s, i, engine):
            a, b = T_PARTS[i]
            load = max(l[0] for l in T_LOADS if l[0] <= a)
            raw = x_raw[s, load]
            xb = keep.tile([P, b - a, 4], BF16, align_bytes=64, name="xb_%d_%d" % (s, a))
            src = raw[:, :, a - load : b - load].rearrange("p j t -> p t j")
            if engine == "v":
                nc.vector.tensor_copy(out=xb[:], in_=src)
            else:
                nc.scalar.copy(out=xb[:], in_=src)
            return xb

        def quantise_x(s, i, xb):
            a, b = T_PARTS[i]
            nc.vector.quantize_mx(
                out=xw[s][:, a:b].bitcast(FP8X4),
                scales=xs[4 * s : P, a:b],
                in_=xb[:].rearrange("p t j -> p (t j)"),
            )

        def gather_words(s, c):
            a, b = CHUNKS[c][0] * C, CHUNKS[c][1] * C
            if s == 0:
                words = gring.tile([P, 3 * C], U32, align_bytes=64, name="words")
            else:
                words = keep.tile([P, b - a], U32, align_bytes=64, name="words1_%d" % c)
            nc.vector.tensor_copy(out=words[:, : b - a], in_=xw[s][:].indirect(offs_t[:, a // 16 : b // 16]))
            for e in range(*CHUNKS[c]):
                gw[s, e] = words[:, e * C - a : (e + 1) * C - a]

        def gather_scales(c):
            a, b = CHUNKS[c][0] * C, CHUNKS[c][1] * C
            nc.vector.tensor_copy(out=gs[:, a:b], in_=xs[:].indirect(offs_t[:, a // 16 : b // 16]))
            if CHUNKS[c][1] in [x[1] for x in SHIFTS.values()]:
                lo = [x for x in SHIFTS.values() if x[1] == CHUNKS[c][1]][0][0] * C
                nc.scalar.dma_start(out=gs1[0:112, lo:b].bitcast(I32), in_=gs[4:116, lo:b].bitcast(I32))

        load_rest()
        for a, b in W_LOADS[1:]:
            load_w1(a, b)
        gates = keep.tile([P, TOP, T], F32, name="gates")
        nc.sync.dma_start(out=gates[:], in_=gate.rearrange("r n t -> n r t"))

        for s, engines in ((0, "svv"), (1, "svv")):
            xbs = [interleave(s, i, engines[i]) for i in range(3)]
            for i in range(3):
                quantise_x(s, i, xbs[i])
            if s == 0:
                gather_words(0, 0)
                gather_words(0, 1)
        gather_scales(0)
        gather_words(1, 0)
        gather_scales(1)
        gather_scales(2)
        gather_words(1, 1)
        gather_words(0, 2)
        gather_words(1, 2)
        gather_words(0, 3)
        gather_scales(3)
        gather_words(1, 3)
        gather_scales(4)
        gather_scales(5)

        y_all = keep.tile([P, S], F32, name="y_all")

        def first_layer(e):
            acc = psum_a.tile([C, H], F32, name="acc")
            w, at = w1[e]
            slots = slice(e * C, (e + 1) * C)
            for s in range(PASSES):
                cols = slice((e * PASSES + s) * H, (e * PASSES + s + 1) * H)
                nc.tensor.matmul_mx(
                    out=acc[:],
                    lhsT=gw[s, e].bitcast(FP8X4),
                    lhsT_scale=(gs, gs1)[s][:, slots],
                    rhs=w[:, at, s, :].bitcast(FP4X4),
                    rhs_scale=w1s[:, cols],
                    start=(s == 0),
                    stop=(s == PASSES - 1),
                )
            h = ring.tile([C, 2, P, 2], BF16, name="h")
            nc.scalar.activation(out=h[:], in_=acc[:].rearrange("c (p u d) -> c u p d", u=2, d=2), func=ACT.Relu)
            return h[:].rearrange("c u p d -> c (u p d)").bitcast(F32)

        def turn(a, b, hb):
            n = b - a
            ht = psum_t.tile([P, n, 2, C], F32, name="ht")
            for e in range(a, b):
                pairs = first_layer(e)
                for u in range(2):
                    nc.tensor.transpose(ht[:, e - a, u, :], pairs[:, u * P : (u + 1) * P], ident[:])
            copy = nc.vector.tensor_copy if a in VECTOR_TURNS else nc.scalar.copy
            copy(
                out=hb.rearrange("p c d -> p (c d)").bitcast(F32).rearrange("p (g c u) -> p g c u", g=n, u=2),
                in_=ht[:].rearrange("p g u c -> p g c u"),
            )

        def second_layer(a, b, hb):
            n = b - a
            hw = keep.tile([P, n * C], U32, align_bytes=64, name="hw_%d" % a)
            hs = keep.tile([P, n * C], U8, align_bytes=64, name="hs_%d" % a)
            nc.vector.quantize_mx(out=hw[:].bitcast(FP8X4), scales=hs[:], in_=hb[:].rearrange("p c d -> p (c d)"))
            y = psum_y.tile([N, n * C], F32, name="y")
            for e in range(a, b):
                cols = slice((e - a) * C, (e - a + 1) * C)
                nc.tensor.matmul_mx(
                    out=y[:, cols],
                    lhsT=w2[:, e, :].bitcast(FP4X4),
                    lhsT_scale=w2s[:, e * N : (e + 1) * N],
                    rhs=hw[:, cols].bitcast(FP8X4),
                    rhs_scale=hs[:, cols],
                    start=True,
                    stop=True,
                )
            nc.scalar.copy(out=y_all[:, a * C : b * C], in_=y[:])

        gathered = 4
        for i, (a, b) in enumerate(BATCHES):
            hb = keep.tile([P, (b - a) * C, 4], BF16, align_bytes=64, name="hb_%d" % a)
            for e in range(a, b, 2):
                f = min(e + 2, b)
                while gathered < len(CHUNKS) and CHUNKS[gathered - 4][1] <= e:
                    gather_words(0, gathered)
                    gather_words(1, gathered)
                    gathered += 1
                turn(e, f, hb[:, (e - a) * C : (f - a) * C, :])
            second_layer(a, b, hb)

        for a, b in OUT_PARTS:
            prods = []
            for r in range(TOP):
                prod = keep.tile([N, b - a], F32, name="prod_%d_%d" % (a, r))
                nc.vector.tensor_tensor(
                    out=prod[:],
                    in0=y_all[:].indirect(pos_t[r][:, a // 16 : b // 16]),
                    in1=gates[:, r, a:b],
                    op=MULT,
                )
                prods.append(prod)
            part = keep.tile([N, b - a], F32, name="part_%d" % a)
            nc.vector.tensor_tensor(out=part[:], in0=prods[0][:], in1=prods[1][:], op=ADD)
            result = keep.tile([N, b - a], F32, name="result_%d" % a)
            nc.vector.tensor_tensor(out=result[:], in0=part[:], in1=prods[2][:], op=ADD)
            nc.sync.dma_start(out=out[:, a:b], in_=result[:])
